import numpy as np
import ml_dtypes


def mxq(x, axis, fmt="e4m3"):
    dtype, down = {"e4m3": (ml_dtypes.float8_e4m3fn, 7), "e5m2": (ml_dtypes.float8_e5m2, 14)}[fmt]
    v = np.moveaxis(np.asarray(x, np.float32).astype(ml_dtypes.bfloat16).astype(np.float64), axis, -1)
    blocks = v.reshape(v.shape[:-1] + (-1, 32))
    amax = np.abs(blocks).max(-1, keepdims=True)
    byte = np.maximum(np.where(amax > 0, np.frexp(amax)[1] - 1 + 127, 0) - down, 1)
    scale = np.exp2(byte - 127.0)
    codes = (blocks / scale).astype(np.float32).astype(dtype).astype(np.float64)
    return np.moveaxis((codes * scale).reshape(v.shape), -1, axis)


WIDE = False


def mx_kscale(k):
    if not WIDE:
        return np.ones(k)
    levels = np.array([10, -10, 5, -5, 0])
    if k % 512:
        return np.exp2(np.random.permutation(np.resize(levels, k // 32))).repeat(32)
    a = np.empty((k // 512, 16))
    for p in range(k // 512):
        a[p, :8] = np.random.permutation(np.resize(levels, 8))
        for g in range(8):
            far = levels[np.abs(levels - a[p, g]) >= 10]
            a[p, g + 8] = far[np.random.randint(len(far))]
    return np.exp2(a.ravel()).repeat(32)


def f64(x):
    return np.asarray(x).astype(np.float64)


def striped(idx):
    return np.tile(idx.reshape(-1, 16).T, (8, 1)).astype(np.uint16)


def unstriped(offs):
    return offs[:16].T.reshape(-1).astype(np.int64)


def pack_weight(w):
    k, n = w.shape
    w = f64(np.asarray(w, np.float32).astype(ml_dtypes.bfloat16)).reshape(k // 32, 32, n)
    amax = np.abs(w).max(1)
    byte = np.clip(np.where(amax > 0, np.frexp(amax)[1] - 1 + 127 - 7, 1), 1, 254)
    scaled = (w * np.exp2(127.0 - byte)[:, None, :]).reshape(k, n).astype(np.float32)
    words = np.ascontiguousarray(scaled.reshape(k // 512, 128, 4, n).transpose(0, 1, 3, 2)).astype(ml_dtypes.float8_e4m3fn).view(np.uint8)
    return words, np.ascontiguousarray(byte.astype(np.uint8).reshape(k // 512, 16, n))


def unpack_weight(words, scales):
    g, p, n, _ = words.shape
    vals = np.ascontiguousarray(words).view(ml_dtypes.float8_e4m3fn).astype(np.float64) * np.repeat(np.exp2(scales.astype(np.float64) - 127.0), 8, axis=1)[..., None]
    return vals.transpose(0, 1, 3, 2).reshape(g * 512, n)


K, T, S, N, H, J, C = 512, 2048, 512, 512, 512, 512, 512


def setup_inputs():
    n = np.random.standard_normal
    s = mx_kscale(K)[:, None]
    u = mx_kscale(S)
    packed_xT = pack_weight(n((K, T)) * s)
    return {
        "x_words": packed_xT[0],
        "x_scales": packed_xT[1],
        "w1": (n((K, H)) / np.sqrt(K) / s).astype(np.float32),
        "tab": n((H, J)).astype(np.float32),
        "gn": (np.random.uniform(0.5, 1.5, (H, 1)) * u[:, None]).astype(np.float32),
        "w2": (n((H, N)) / np.sqrt(H) / u[:, None]).astype(np.float32),
        "gs": (np.random.uniform(0.5, 1.5, (K, 1)) / s).astype(np.float32),
        "offs": striped(np.random.permutation(T)[:S]),
        "n1": striped(np.random.randint(0, J, S)),
        "n2": striped(np.random.permutation(S)),
        "n3": striped(np.random.permutation(S)),
        "n4": striped(np.random.permutation(S)),
        "n5": striped(np.random.permutation(S)),
        "cand": striped(np.random.permutation(T)[:C]),
        "n6": striped(np.random.permutation(S)),
        "n7": striped(np.random.permutation(S)),
    }


def reference(x_words, x_scales, w1, tab, gn, w2, gs, offs, n1, n2, n3, n4, n5, cand, n6, n7):
    xq = unpack_weight(x_words, x_scales)[:, unstriped(offs)]
    y = mxq(f64(w1), 0, "e4m3").T @ xq
    z = f64(gn) * (np.abs(y - y[:, unstriped(n2)] - f64(tab)[:, unstriped(n1)]))
    a = mxq(f64(w2), 0, "e4m3").T @ mxq(z, 0, "e4m3")
    x_cand = unpack_weight(x_words, x_scales)[:, unstriped(cand)]
    z2 = f64(gs) * (0.75 * (y * y[:, unstriped(n3)] + y[:, unstriped(n4)] * y[:, unstriped(n5)]))
    b = 0.0625 * ((x_cand.T @ mxq(z2, 0, "e4m3")))
    return np.maximum(a, b[:, unstriped(n7)]) - (np.minimum(a[:, unstriped(n6)], b))

@@ -1,0 +1,184 @@
+from contextlib import ExitStack
+
+import concourse.mybir as mybir
+
+F32 = mybir.dt.float32
+BF16 = mybir.dt.bfloat16
+I32 = mybir.dt.int32
+U32 = mybir.dt.uint32
+U16 = mybir.dt.uint16
+U8 = mybir.dt.uint8
+FP8X4 = mybir.dt.float8_e4m3fn_x4
+ALU = mybir.AluOpType
+ACT = mybir.ActivationFunctionType
+
+P = 128
+PACK = 4
+T = 2048
+S = 512
+SPARE = 8
+FLOPS = 3 * 2 * 512 * 512 * 512
+
+
+def tile_picked_fkcdmaxbkindddot_none_p_kernel(
+    tc, x_words, x_scales, w1, tab, gn, w2, gs, offs, n1, n2, n3, n4, n5, cand, n6, n7, out
+):
+    nc = tc.nc
+    with ExitStack() as ctx:
+        lists = ctx.enter_context(tc.tile_pool(name="lists", bufs=1))
+        keep = ctx.enter_context(tc.tile_pool(name="keep", bufs=1))
+        psum = ctx.enter_context(tc.psum_pool(name="psum", bufs=1))
+
+        def load_list(name, src):
+            tile = lists.tile([P, S // 16], U16, name=name)
+            nc.sync.dma_start(tile[:], src)
+            return tile
+
+        def windows(name):
+            tiles = [keep.tile([P, S + SPARE], F32, name="%s%d" % (name, t)) for t in range(PACK)]
+            for tile in tiles:
+                nc.gpsimd.memset(tile[:, S:], 0.0)
+            return tiles
+
+        def planes(name):
+            return keep.tile([P, PACK, S], F32, name=name, tag=name, align_bytes=64)
+
+        def woven_in(src):
+            return src.rearrange("p t (c i) -> p c t i", i=4)
+
+        def woven_out(dst):
+            return dst.rearrange("p (c i t) -> p c t i", i=4, t=PACK)
+
+        def quantize(name, values, width, tag=""):
+            codes = keep.tile([P, width], U32, name=name + "_codes", tag=tag, align_bytes=64)
+            scales = keep.tile([P, width], U8, name=name + "_scales", align_bytes=64)
+            nc.vector.quantize_mx(out=codes[:].bitcast(FP8X4), scales=scales[:], in_=values)
+            return codes, scales
+
+        def product(bank, lhs, cols, rhs):
+            nc.tensor.matmul_mx(
+                out=bank[:], lhsT=lhs[0][:, cols].bitcast(FP8X4), lhsT_scale=lhs[1][:, cols],
+                rhs=rhs[0][:].bitcast(FP8X4), rhs_scale=rhs[1][:], start=True, stop=True,
+            )
+
+        xs = keep.tile([P, T], U8, name="xs", align_bytes=64)
+        nc.gpsimd.memset(xs[:].bitcast(I32), 0)
+        l_offs = load_list("l_offs", offs)
+        l_cand = load_list("l_cand", cand)
+        for q in range(4):
+            nc.sync.dma_start(xs[32 * q : 32 * q + 4, :].bitcast(I32), x_scales[0, 4 * q : 4 * q + 4, :].bitcast(I32))
+        w1_raw = planes("w1_raw")
+        nc.sync.dma_start(w1_raw[:], w1.rearrange("(p j) c -> p j c", j=PACK))
+        xw = keep.tile([P, T], I32, name="xw", align_bytes=64)
+        nc.sync.dma_start(xw[:], x_words[0].rearrange("p n t -> p (n t)").bitcast(I32))
+        gs_sb = keep.tile([P, PACK], F32, name="gs_sb")
+        nc.sync.dma_start(gs_sb[:], gs.rearrange("(p t) o -> p (t o)", t=PACK))
+        l_n4 = load_list("l_n4", n4)
+        l_n3 = load_list("l_n3", n3)
+        l_n5 = load_list("l_n5", n5)
+        l_n1 = load_list("l_n1", n1)
+        tab_w = windows("tab_w")
+        tab_rows = tab.rearrange("(p t) c -> t p c", t=PACK)
+        for t in range(PACK):
+            nc.sync.dma_start(tab_w[t][:, :S], tab_rows[t])
+        l_n2 = load_list("l_n2", n2)
+        gn_sb = keep.tile([P, PACK], F32, name="gn_sb")
+        nc.sync.dma_start(gn_sb[:], gn.rearrange("(p t) o -> p (t o)", t=PACK))
+        w2_raw = planes("w2_raw")
+        nc.sync.dma_start(w2_raw[:], w2.rearrange("(p j) c -> p j c", j=PACK))
+        l_n7 = load_list("l_n7", n7)
+        l_n6 = load_list("l_n6", n6)
+
+        y_w = windows("y_w")
+        ys_w = windows("ys_w")
+        b_w = windows("b_w")
+        a_w = windows("a_w")
+
+        def pick(name, offsets, window, dtype):
+            tile = keep.tile([P, S], dtype, name=name, align_bytes=64)
+            nc.vector.tensor_copy(tile[:], window.indirect(offsets[:]))
+            return tile
+
+        xq_scales = pick("xq_scales", l_offs, xs[:], U8)
+        xc_scales = pick("xc_scales", l_cand, xs[:], U8)
+        w1_dealt = w1_raw[:].rearrange("p j (m t) -> p m j t", t=PACK)
+        w1_q = []
+        for half in range(2):
+            w1_bf = keep.tile([P, 2 * P * PACK], BF16, name="w1_bf%d" % half, align_bytes=64)
+            dst = w1_bf[:].rearrange("p (t m j) -> p m j t", t=2, j=PACK)
+            src = w1_dealt[:, :, :, 2 * half : 2 * half + 2]
+            if half == 0:
+                nc.vector.tensor_copy(dst, src)
+            else:
+                nc.scalar.copy(dst, src)
+            w1_q.append(quantize("w1_%d" % half, w1_bf[:], 2 * P))
+        xq = (pick("xq_words", l_offs, xw[:].bitcast(U32), U32), xq_scales)
+        y_ps = [psum.tile([P, S], F32, name="y_ps%d" % t, tag="bank%d" % t) for t in range(PACK)]
+        for t in range(PACK):
+            product(y_ps[t], w1_q[t // 2], slice((t % 2) * P, (t % 2 + 1) * P), xq)
+        xc = (pick("xc_words", l_cand, xw[:].bitcast(U32), U32), xc_scales)
+
+        g4 = planes("g4")
+        p1 = planes("p1")
+        p2 = planes("p2")
+        g1 = planes("g1")
+        gain2 = keep.tile([P, PACK], F32, name="gain2")
+        nc.gpsimd.tensor_scalar(gain2[:], gs_sb[:], 0.75, 0.0, ALU.mult, ALU.add)
+        for t in range(PACK):
+            nc.scalar.copy(y_w[t][:, :S], y_ps[t][:])
+            if t < 2:
+                nc.vector.tensor_scalar(ys_w[t][:, :S], y_w[t][:, :S], gain2[:, t : t + 1], None, ALU.mult)
+            else:
+                nc.scalar.activation(ys_w[t][:, :S], y_ps[t][:], ACT.Copy, scale=gain2[:, t : t + 1])
+            nc.scalar.activation(g4[:, t, :], ys_w[t][:].indirect(l_n4[:]), ACT.Copy)
+            nc.vector.tensor_tensor(p1[:, t, :], y_w[t][:].indirect(l_n3[:]), ys_w[t][:, :S], ALU.mult)
+            nc.vector.tensor_tensor(p2[:, t, :], y_w[t][:].indirect(l_n5[:]), g4[:, t, :], ALU.mult)
+        z2_bf = keep.tile([P, S * PACK], BF16, name="z2_bf", align_bytes=64)
+        nc.vector.tensor_tensor(woven_out(z2_bf[:]), woven_in(p1[:]), woven_in(p2[:]), ALU.add)
+        z2_q = quantize("z2", z2_bf[:], S)
+        for t in range(PACK):
+            nc.scalar.activation(g1[:, t, :], tab_w[t][:].indirect(l_n1[:]), ACT.Copy)
+        w2_bf = keep.tile([P, S * PACK], BF16, name="w2_bf", align_bytes=64)
+        for quarter in range(4):
+            cs = slice(32 * quarter, 32 * (quarter + 1))
+            nc.scalar.copy(woven_out(w2_bf[:])[:, cs], woven_in(w2_raw[:])[:, cs])
+        b_ps = [psum.tile([P, S], F32, name="b_ps%d" % t, tag="bank%d" % (PACK + t)) for t in range(PACK)]
+        for t in range(PACK):
+            product(b_ps[t], xc, slice(t * P, (t + 1) * P), z2_q)
+
+        nd = p1
+        e = planes("e")
+        mag = planes("mag")
+        g7 = planes("g7")
+        for t in range(PACK):
+            nc.vector.tensor_tensor(nd[:, t, :], g1[:, t, :], y_ps[t][:], ALU.subtract)
+            nc.vector.tensor_tensor(e[:, t, :], y_w[t][:].indirect(l_n2[:]), nd[:, t, :], ALU.add)
+            nc.scalar.activation(mag[:, t, :], e[:, t, :], ACT.Abs)
+        w2_q = quantize("w2", w2_bf[:], S, tag="p1")
+        for t in range(PACK):
+            nc.scalar.activation(b_w[t][:, :S], b_ps[t][:], ACT.Copy, scale=0.0625)
+            nc.scalar.activation(g7[:, t, :], b_w[t][:].indirect(l_n7[:]), ACT.Copy)
+        z_bf = keep.tile([P, S * PACK], BF16, name="z_bf", align_bytes=64)
+        gn_wide = gn_sb[:].unsqueeze(1).unsqueeze(3).to_broadcast([P, S // 4, PACK, 4])
+        nc.vector.tensor_tensor(woven_out(z_bf[:]), woven_in(mag[:]), gn_wide, ALU.mult)
+        z_q = quantize("z", z_bf[:], S)
+        a_ps = [psum.tile([P, S], F32, name="a_ps%d" % t, tag="bank%d" % t) for t in range(PACK)]
+        for t in range(PACK):
+            product(a_ps[t], w2_q, slice(t * P, (t + 1) * P), z_q)
+
+        g6 = planes("g6")
+        hi = planes("hi")
+        lo = planes("lo")
+        res = planes("res")
+        for t in (1, 3):
+            nc.vector.tensor_copy(a_w[t][:, :S], a_ps[t][:])
+        for t in range(PACK):
+            if t % 2 == 0:
+                nc.scalar.copy(a_w[t][:, :S], a_ps[t][:])
+            nc.scalar.activation(g6[:, t, :], a_w[t][:].indirect(l_n6[:]), ACT.Copy)
+        for t in range(PACK):
+            nc.vector.tensor_tensor(hi[:, t, :], g7[:, t, :], a_ps[t][:], ALU.max)
+            nc.vector.scalar_tensor_tensor(lo[:, t, :], b_ps[t][:], 0.0625, g6[:, t, :], ALU.mult, ALU.min)
+            engine = nc.gpsimd if t < PACK - 1 else nc.vector
+            engine.tensor_tensor(res[:, t, :], hi[:, t, :], lo[:, t, :], ALU.subtract)
+            nc.sync.dma_start(out[t * P : (t + 1) * P, :], res[:, t, :])

@@ -16,6 +16,7 @@ P = 128
 PACK = 4
 T = 2048
 S = 512
+HALF = S // 2
 SPARE = 8
 FLOPS = 3 * 2 * 512 * 512 * 512
 
@@ -57,7 +58,7 @@ def tile_picked_fkcdmaxbkindddot_none_p_kernel(
 
         def product(bank, lhs, cols, rhs):
             nc.tensor.matmul_mx(
-                out=bank[:], lhsT=lhs[0][:, cols].bitcast(FP8X4), lhsT_scale=lhs[1][:, cols],
+                out=bank, lhsT=lhs[0][:, cols].bitcast(FP8X4), lhsT_scale=lhs[1][:, cols],
                 rhs=rhs[0][:].bitcast(FP8X4), rhs_scale=rhs[1][:], start=True, stop=True,
             )
 
@@ -115,7 +116,7 @@ def tile_picked_fkcdmaxbkindddot_none_p_kernel(
         xq = (pick("xq_words", l_offs, xw[:].bitcast(U32), U32), xq_scales)
         y_ps = [psum.tile([P, S], F32, name="y_ps%d" % t, tag="bank%d" % t) for t in range(PACK)]
         for t in range(PACK):
-            product(y_ps[t], w1_q[t // 2], slice((t % 2) * P, (t % 2 + 1) * P), xq)
+            product(y_ps[t][:], w1_q[t // 2], slice((t % 2) * P, (t % 2 + 1) * P), xq)
         xc = (pick("xc_words", l_cand, xw[:].bitcast(U32), U32), xc_scales)
 
         g4 = planes("g4")
@@ -144,41 +145,72 @@ def tile_picked_fkcdmaxbkindddot_none_p_kernel(
             nc.scalar.copy(woven_out(w2_bf[:])[:, cs], woven_in(w2_raw[:])[:, cs])
         b_ps = [psum.tile([P, S], F32, name="b_ps%d" % t, tag="bank%d" % (PACK + t)) for t in range(PACK)]
         for t in range(PACK):
-            product(b_ps[t], xc, slice(t * P, (t + 1) * P), z2_q)
+            product(b_ps[t][:], xc, slice(t * P, (t + 1) * P), z2_q)
 
+        half_cols = [slice(0, HALF), slice(HALF, S)]
+        half_list = [slice(0, HALF // 16), slice(HALF // 16, S // 16)]
+        last = PACK - 1
         nd = p1
         e = planes("e")
-        mag = planes("mag")
-        g7 = planes("g7")
+        mag = keep.tile([P, 2, PACK, HALF], F32, name="mag", align_bytes=64)
         for t in range(PACK):
             nc.vector.tensor_tensor(nd[:, t, :], g1[:, t, :], y_ps[t][:], ALU.subtract)
-            nc.vector.tensor_tensor(e[:, t, :], y_w[t][:].indirect(l_n2[:]), nd[:, t, :], ALU.add)
-            nc.scalar.activation(mag[:, t, :], e[:, t, :], ACT.Abs)
+            if t < last:
+                nc.vector.tensor_tensor(e[:, t, :], y_w[t][:].indirect(l_n2[:]), nd[:, t, :], ALU.add)
+                nc.scalar.activation(mag[:, :, t, :], e[:, t, :].rearrange("p (h c) -> p h c", h=2), ACT.Abs)
+            else:
+                for h in range(2):
+                    nc.vector.tensor_tensor(
+                        e[:, t, half_cols[h]], y_w[t][:].indirect(l_n2[:, half_list[h]]), nd[:, t, half_cols[h]], ALU.add
+                    )
+                    nc.scalar.activation(mag[:, h, t, :], e[:, t, half_cols[h]], ACT.Abs)
         w2_q = quantize("w2", w2_bf[:], S, tag="p1")
+        g7_early = keep.tile([P, 2, S], F32, name="g7_early")
+        g7_late = keep.tile([P, 2, S], F32, name="g7_late", tag="e", align_bytes=64)
+        g7 = [g7_early[:, 0, :], g7_early[:, 1, :], g7_late[:, 0, :], g7_late[:, 1, :]]
         for t in range(PACK):
             nc.scalar.activation(b_w[t][:, :S], b_ps[t][:], ACT.Copy, scale=0.0625)
-            nc.scalar.activation(g7[:, t, :], b_w[t][:].indirect(l_n7[:]), ACT.Copy)
-        z_bf = keep.tile([P, S * PACK], BF16, name="z_bf", align_bytes=64)
-        gn_wide = gn_sb[:].unsqueeze(1).unsqueeze(3).to_broadcast([P, S // 4, PACK, 4])
-        nc.vector.tensor_tensor(woven_out(z_bf[:]), woven_in(mag[:]), gn_wide, ALU.mult)
-        z_q = quantize("z", z_bf[:], S)
-        a_ps = [psum.tile([P, S], F32, name="a_ps%d" % t, tag="bank%d" % t) for t in range(PACK)]
-        for t in range(PACK):
-            product(a_ps[t], w2_q, slice(t * P, (t + 1) * P), z_q)
+            nc.scalar.activation(g7[t], b_w[t][:].indirect(l_n7[:]), ACT.Copy)
+        z_bf = keep.tile([P, HALF * PACK], BF16, name="z_bf", tag="z_bf", align_bytes=64)
+        gn_wide = gn_sb[:].unsqueeze(1).unsqueeze(3).to_broadcast([P, HALF // 4, PACK, 4])
+        a_banks = [psum.tile([P, 2, HALF], F32, name="a_bank%d" % k, tag="bank%d" % k) for k in range(PACK)]
+        a_ps = [[a_banks[2 * h + t // 2][:, t % 2, :] for t in range(PACK)] for h in range(2)]
+        for h in range(2):
+            nc.vector.tensor_tensor(woven_out(z_bf[:]), woven_in(mag[:, h]), gn_wide, ALU.mult)
+            z_q = quantize("z%d" % h, z_bf[:], HALF)
+            for t in range(PACK):
+                product(a_ps[h][t], w2_q, slice(t * P, (t + 1) * P), z_q)
+        hi = keep.tile([P, PACK, S], F32, name="hi", tag="z_bf", align_bytes=64)
+        for h in range(2):
+            for t in range(PACK):
+                if h == 0 or t == 0:
+                    nc.scalar.copy(a_w[t][:, half_cols[h]], a_ps[h][t])
+                else:
+                    nc.vector.tensor_copy(a_w[t][:, half_cols[h]], a_ps[h][t])
+            for t in range(PACK):
+                if h == 0:
+                    nc.vector.tensor_tensor(hi[:, t, half_cols[h]], g7[t][:, half_cols[h]], a_ps[h][t], ALU.max)
 
         g6 = planes("g6")
-        hi = planes("hi")
         lo = planes("lo")
         res = planes("res")
-        for t in (1, 3):
-            nc.vector.tensor_copy(a_w[t][:, :S], a_ps[t][:])
         for t in range(PACK):
-            if t % 2 == 0:
-                nc.scalar.copy(a_w[t][:, :S], a_ps[t][:])
-            nc.scalar.activation(g6[:, t, :], a_w[t][:].indirect(l_n6[:]), ACT.Copy)
-        for t in range(PACK):
-            nc.vector.tensor_tensor(hi[:, t, :], g7[:, t, :], a_ps[t][:], ALU.max)
-            nc.vector.scalar_tensor_tensor(lo[:, t, :], b_ps[t][:], 0.0625, g6[:, t, :], ALU.mult, ALU.min)
-            engine = nc.gpsimd if t < PACK - 1 else nc.vector
-            engine.tensor_tensor(res[:, t, :], hi[:, t, :], lo[:, t, :], ALU.subtract)
-            nc.sync.dma_start(out[t * P : (t + 1) * P, :], res[:, t, :])
+            rows = slice(t * P, (t + 1) * P)
+            nc.vector.tensor_tensor(hi[:, t, half_cols[1]], g7[t][:, half_cols[1]], a_ps[1][t], ALU.max)
+            if t < last:
+                nc.scalar.activation(g6[:, t, :], a_w[t][:].indirect(l_n6[:]), ACT.Copy)
+                nc.vector.scalar_tensor_tensor(lo[:, t, :], b_ps[t][:], 0.0625, g6[:, t, :], ALU.mult, ALU.min)
+                if t < 2:
+                    nc.gpsimd.tensor_tensor(res[:, t, :], hi[:, t, :], lo[:, t, :], ALU.subtract)
+                else:
+                    for h, engine in enumerate((nc.gpsimd, nc.vector)):
+                        cols = half_cols[h]
+                        engine.tensor_tensor(res[:, t, cols], hi[:, t, cols], lo[:, t, cols], ALU.subtract)
+                nc.sync.dma_start(out[rows, :], res[:, t, :])
+            else:
+                for h in range(2):
+                    cols = half_cols[h]
+                    nc.scalar.activation(g6[:, t, cols], a_w[t][:].indirect(l_n6[:, half_list[h]]), ACT.Copy)
+                    nc.vector.scalar_tensor_tensor(lo[:, t, cols], b_ps[t][:, cols], 0.0625, g6[:, t, cols], ALU.mult, ALU.min)
+                    nc.vector.tensor_tensor(res[:, t, cols], hi[:, t, cols], lo[:, t, cols], ALU.subtract)
+                    nc.sync.dma_start(out[rows, cols], res[:, t, cols])

from contextlib import ExitStack

import concourse.mybir as mybir

F32 = mybir.dt.float32
BF16 = mybir.dt.bfloat16
I32 = mybir.dt.int32
U32 = mybir.dt.uint32
U16 = mybir.dt.uint16
U8 = mybir.dt.uint8
FP8X4 = mybir.dt.float8_e4m3fn_x4
ALU = mybir.AluOpType
ACT = mybir.ActivationFunctionType

P = 128
PACK = 4
T = 2048
S = 512
HALF = S // 2
SPARE = 8
FLOPS = 3 * 2 * 512 * 512 * 512


def tile_picked_fkcdmaxbkindddot_none_p_kernel(
    tc, x_words, x_scales, w1, tab, gn, w2, gs, offs, n1, n2, n3, n4, n5, cand, n6, n7, out
):
    nc = tc.nc
    with ExitStack() as ctx:
        lists = ctx.enter_context(tc.tile_pool(name="lists", bufs=1))
        keep = ctx.enter_context(tc.tile_pool(name="keep", bufs=1))
        psum = ctx.enter_context(tc.psum_pool(name="psum", bufs=1))

        def load_list(name, src):
            tile = lists.tile([P, S // 16], U16, name=name)
            nc.sync.dma_start(tile[:], src)
            return tile

        def windows(name):
            tiles = [keep.tile([P, S + SPARE], F32, name="%s%d" % (name, t)) for t in range(PACK)]
            for tile in tiles:
                nc.gpsimd.memset(tile[:, S:], 0.0)
            return tiles

        def planes(name):
            return keep.tile([P, PACK, S], F32, name=name, tag=name, align_bytes=64)

        def woven_in(src):
            return src.rearrange("p t (c i) -> p c t i", i=4)

        def woven_out(dst):
            return dst.rearrange("p (c i t) -> p c t i", i=4, t=PACK)

        def quantize(name, values, width, tag=""):
            codes = keep.tile([P, width], U32, name=name + "_codes", tag=tag, align_bytes=64)
            scales = keep.tile([P, width], U8, name=name + "_scales", align_bytes=64)
            nc.vector.quantize_mx(out=codes[:].bitcast(FP8X4), scales=scales[:], in_=values)
            return codes, scales

        def product(bank, lhs, cols, rhs):
            nc.tensor.matmul_mx(
                out=bank, lhsT=lhs[0][:, cols].bitcast(FP8X4), lhsT_scale=lhs[1][:, cols],
                rhs=rhs[0][:].bitcast(FP8X4), rhs_scale=rhs[1][:], start=True, stop=True,
            )

        xs = keep.tile([P, T], U8, name="xs", align_bytes=64)
        nc.gpsimd.memset(xs[:].bitcast(I32), 0)
        l_offs = load_list("l_offs", offs)
        l_cand = load_list("l_cand", cand)
        for q in range(4):
            nc.sync.dma_start(xs[32 * q : 32 * q + 4, :].bitcast(I32), x_scales[0, 4 * q : 4 * q + 4, :].bitcast(I32))
        w1_raw = planes("w1_raw")
        nc.sync.dma_start(w1_raw[:], w1.rearrange("(p j) c -> p j c", j=PACK))
        xw = keep.tile([P, T], I32, name="xw", align_bytes=64)
        nc.sync.dma_start(xw[:], x_words[0].rearrange("p n t -> p (n t)").bitcast(I32))
        gs_sb = keep.tile([P, PACK], F32, name="gs_sb")
        nc.sync.dma_start(gs_sb[:], gs.rearrange("(p t) o -> p (t o)", t=PACK))
        l_n4 = load_list("l_n4", n4)
        l_n3 = load_list("l_n3", n3)
        l_n5 = load_list("l_n5", n5)
        l_n1 = load_list("l_n1", n1)
        tab_w = windows("tab_w")
        tab_rows = tab.rearrange("(p t) c -> t p c", t=PACK)
        for t in range(PACK):
            nc.sync.dma_start(tab_w[t][:, :S], tab_rows[t])
        l_n2 = load_list("l_n2", n2)
        gn_sb = keep.tile([P, PACK], F32, name="gn_sb")
        nc.sync.dma_start(gn_sb[:], gn.rearrange("(p t) o -> p (t o)", t=PACK))
        w2_raw = planes("w2_raw")
        nc.sync.dma_start(w2_raw[:], w2.rearrange("(p j) c -> p j c", j=PACK))
        l_n7 = load_list("l_n7", n7)
        l_n6 = load_list("l_n6", n6)

        y_w = windows("y_w")
        ys_w = windows("ys_w")
        b_w = windows("b_w")
        a_w = windows("a_w")

        def pick(name, offsets, window, dtype):
            tile = keep.tile([P, S], dtype, name=name, align_bytes=64)
            nc.vector.tensor_copy(tile[:], window.indirect(offsets[:]))
            return tile

        xq_scales = pick("xq_scales", l_offs, xs[:], U8)
        xc_scales = pick("xc_scales", l_cand, xs[:], U8)
        w1_dealt = w1_raw[:].rearrange("p j (m t) -> p m j t", t=PACK)
        w1_q = []
        for half in range(2):
            w1_bf = keep.tile([P, 2 * P * PACK], BF16, name="w1_bf%d" % half, align_bytes=64)
            dst = w1_bf[:].rearrange("p (t m j) -> p m j t", t=2, j=PACK)
            src = w1_dealt[:, :, :, 2 * half : 2 * half + 2]
            if half == 0:
                nc.vector.tensor_copy(dst, src)
            else:
                nc.scalar.copy(dst, src)
            w1_q.append(quantize("w1_%d" % half, w1_bf[:], 2 * P))
        xq = (pick("xq_words", l_offs, xw[:].bitcast(U32), U32), xq_scales)
        y_ps = [psum.tile([P, S], F32, name="y_ps%d" % t, tag="bank%d" % t) for t in range(PACK)]
        for t in range(PACK):
            product(y_ps[t][:], w1_q[t // 2], slice((t % 2) * P, (t % 2 + 1) * P), xq)
        xc = (pick("xc_words", l_cand, xw[:].bitcast(U32), U32), xc_scales)

        g4 = planes("g4")
        p1 = planes("p1")
        p2 = planes("p2")
        g1 = planes("g1")
        gain2 = keep.tile([P, PACK], F32, name="gain2")
        nc.gpsimd.tensor_scalar(gain2[:], gs_sb[:], 0.75, 0.0, ALU.mult, ALU.add)
        for t in range(PACK):
            nc.scalar.copy(y_w[t][:, :S], y_ps[t][:])
            if t < 2:
                nc.vector.tensor_scalar(ys_w[t][:, :S], y_w[t][:, :S], gain2[:, t : t + 1], None, ALU.mult)
            else:
                nc.scalar.activation(ys_w[t][:, :S], y_ps[t][:], ACT.Copy, scale=gain2[:, t : t + 1])
            nc.scalar.activation(g4[:, t, :], ys_w[t][:].indirect(l_n4[:]), ACT.Copy)
            nc.vector.tensor_tensor(p1[:, t, :], y_w[t][:].indirect(l_n3[:]), ys_w[t][:, :S], ALU.mult)
            nc.vector.tensor_tensor(p2[:, t, :], y_w[t][:].indirect(l_n5[:]), g4[:, t, :], ALU.mult)
        z2_bf = keep.tile([P, S * PACK], BF16, name="z2_bf", align_bytes=64)
        nc.vector.tensor_tensor(woven_out(z2_bf[:]), woven_in(p1[:]), woven_in(p2[:]), ALU.add)
        z2_q = quantize("z2", z2_bf[:], S)
        for t in range(PACK):
            nc.scalar.activation(g1[:, t, :], tab_w[t][:].indirect(l_n1[:]), ACT.Copy)
        w2_bf = keep.tile([P, S * PACK], BF16, name="w2_bf", align_bytes=64)
        for quarter in range(4):
            cs = slice(32 * quarter, 32 * (quarter + 1))
            nc.scalar.copy(woven_out(w2_bf[:])[:, cs], woven_in(w2_raw[:])[:, cs])
        b_ps = [psum.tile([P, S], F32, name="b_ps%d" % t, tag="bank%d" % (PACK + t)) for t in range(PACK)]
        for t in range(PACK):
            product(b_ps[t][:], xc, slice(t * P, (t + 1) * P), z2_q)

        half_cols = [slice(0, HALF), slice(HALF, S)]
        half_list = [slice(0, HALF // 16), slice(HALF // 16, S // 16)]
        last = PACK - 1
        nd = p1
        e = planes("e")
        mag = keep.tile([P, 2, PACK, HALF], F32, name="mag", align_bytes=64)
        for t in range(PACK):
            nc.vector.tensor_tensor(nd[:, t, :], g1[:, t, :], y_ps[t][:], ALU.subtract)
            if t < last:
                nc.vector.tensor_tensor(e[:, t, :], y_w[t][:].indirect(l_n2[:]), nd[:, t, :], ALU.add)
                nc.scalar.activation(mag[:, :, t, :], e[:, t, :].rearrange("p (h c) -> p h c", h=2), ACT.Abs)
            else:
                for h in range(2):
                    nc.vector.tensor_tensor(
                        e[:, t, half_cols[h]], y_w[t][:].indirect(l_n2[:, half_list[h]]), nd[:, t, half_cols[h]], ALU.add
                    )
                    nc.scalar.activation(mag[:, h, t, :], e[:, t, half_cols[h]], ACT.Abs)
        w2_q = quantize("w2", w2_bf[:], S, tag="p1")
        g7_early = keep.tile([P, 2, S], F32, name="g7_early")
        g7_late = keep.tile([P, 2, S], F32, name="g7_late", tag="e", align_bytes=64)
        g7 = [g7_early[:, 0, :], g7_early[:, 1, :], g7_late[:, 0, :], g7_late[:, 1, :]]
        for t in range(PACK):
            nc.scalar.activation(b_w[t][:, :S], b_ps[t][:], ACT.Copy, scale=0.0625)
            nc.scalar.activation(g7[t], b_w[t][:].indirect(l_n7[:]), ACT.Copy)
        z_bf = keep.tile([P, HALF * PACK], BF16, name="z_bf", tag="z_bf", align_bytes=64)
        gn_wide = gn_sb[:].unsqueeze(1).unsqueeze(3).to_broadcast([P, HALF // 4, PACK, 4])
        a_banks = [psum.tile([P, 2, HALF], F32, name="a_bank%d" % k, tag="bank%d" % k) for k in range(PACK)]
        a_ps = [[a_banks[2 * h + t // 2][:, t % 2, :] for t in range(PACK)] for h in range(2)]
        for h in range(2):
            nc.vector.tensor_tensor(woven_out(z_bf[:]), woven_in(mag[:, h]), gn_wide, ALU.mult)
            z_q = quantize("z%d" % h, z_bf[:], HALF)
            for t in range(PACK):
                product(a_ps[h][t], w2_q, slice(t * P, (t + 1) * P), z_q)
        hi = keep.tile([P, PACK, S], F32, name="hi", tag="z_bf", align_bytes=64)
        for h in range(2):
            for t in range(PACK):
                if h == 0 or t == 0:
                    nc.scalar.copy(a_w[t][:, half_cols[h]], a_ps[h][t])
                else:
                    nc.vector.tensor_copy(a_w[t][:, half_cols[h]], a_ps[h][t])
            for t in range(PACK):
                if h == 0:
                    nc.vector.tensor_tensor(hi[:, t, half_cols[h]], g7[t][:, half_cols[h]], a_ps[h][t], ALU.max)

        g6 = planes("g6")
        lo = planes("lo")
        res = planes("res")
        for t in range(PACK):
            rows = slice(t * P, (t + 1) * P)
            nc.vector.tensor_tensor(hi[:, t, half_cols[1]], g7[t][:, half_cols[1]], a_ps[1][t], ALU.max)
            if t < last:
                nc.scalar.activation(g6[:, t, :], a_w[t][:].indirect(l_n6[:]), ACT.Copy)
                nc.vector.scalar_tensor_tensor(lo[:, t, :], b_ps[t][:], 0.0625, g6[:, t, :], ALU.mult, ALU.min)
                if t < 2:
                    nc.gpsimd.tensor_tensor(res[:, t, :], hi[:, t, :], lo[:, t, :], ALU.subtract)
                else:
                    for h, engine in enumerate((nc.gpsimd, nc.vector)):
                        cols = half_cols[h]
                        engine.tensor_tensor(res[:, t, cols], hi[:, t, cols], lo[:, t, cols], ALU.subtract)
                nc.sync.dma_start(out[rows, :], res[:, t, :])
            else:
                for h in range(2):
                    cols = half_cols[h]
                    nc.scalar.activation(g6[:, t, cols], a_w[t][:].indirect(l_n6[:, half_list[h]]), ACT.Copy)
                    nc.vector.scalar_tensor_tensor(lo[:, t, cols], b_ps[t][:, cols], 0.0625, g6[:, t, cols], ALU.mult, ALU.min)
                    nc.vector.tensor_tensor(res[:, t, cols], hi[:, t, cols], lo[:, t, cols], ALU.subtract)
                    nc.sync.dma_start(out[rows, cols], res[:, t, cols])
